import numpy as np, ml_dtypes
CORES = [78,86,94,102,110,118]
N = 6
import mx_ref
NC, G = 256, 4
C = np.float32(0.01184)
BF = ml_dtypes.bfloat16
def cut(t, i, w=512):
    return t[:, w * i:w * i + w]
def tile(rs):
    return np.stack(rs, axis=2).reshape(128, -1).astype(BF)
def layer(w, X):
    out = []
    for i in range(G):
        for t in range(len(X)):
            p = mx_ref.matmul(mx_ref.quantize(cut(w, len(X) * i + t)), X[t])
            z = p if t == 0 else z + p
        out.append(z)
    return out
def act(Z):
    return [np.maximum(z, 0) * C for z in Z]
def setup_inputs(rng):
    def f(*shape):
        return mx_ref.flush((rng.standard_normal(shape, dtype=np.float32) * np.exp2(rng.integers(-2, 3, shape[:-1] + (1,)))).astype(BF))
    return {"x": f(N, 128, N * 4 * NC), "w1": f(N, 128, G * 512), "w2": f(N, 128, 2 * 512)}
def setup_inputs_blocks(rng):
    d = setup_inputs(rng)
    for k in ("x", "w1", "w2"): d[k] = mx_ref.spread(d[k], rng, 4)
    return d
def setup_inputs_wide(rng):
    d = setup_inputs(rng)
    for k in ("x", "w1", "w2"): d[k] = mx_ref.flush((d[k].astype(np.float32) * np.exp2(rng.integers(-6, 7, (N, 1, 1))).astype(np.float32)).astype(BF))
    return d
def reference(x, w1, w2, own=None):
    h = np.zeros((N, 128, 4 * NC), BF)
    for c in range(N):
        for j in range(N):
            P = layer(w1[j], [mx_ref.quantize(cut(x[j], c, 4 * NC))])
            Z = P if j == 0 else [z + p for z, p in zip(Z, P)]
        h[c] = tile(act(Z))
    use = h if own is None else own["h"]
    H = [mx_ref.quantize(use[j]) for j in range(N)]
    y = np.zeros((N, 128, NC), np.float32)
    for r in range(N):
        y[r] = mx_ref.matmul(mx_ref.quantize(cut(w2[r], 0)), H[r]) + mx_ref.matmul(mx_ref.quantize(cut(w2[r], 1)), H[(r + 1) % N])
    return {"h": h, "y": y}

from concourse.bass import DstId, RemoteDMATransfer
from concourse.mybir import dt, AluOpType, ActivationFunctionType

NC = 256
CACT = 0.01184

SCRATCH = {
    "w1b": ("sbuf", [128, 2048], "bfloat16"),
    "xb": ("sbuf", [128, 6144], "bfloat16"),
    "w2b": ("sbuf", [128, 1024], "bfloat16"),
    "w1q": ("sbuf", [128, 512], "float8_e4m3fn_x4"),
    "w1s": ("sbuf", [128, 512], "uint8"),
    "xq": ("sbuf", [128, 1536], "float8_e4m3fn_x4"),
    "xs": ("sbuf", [128, 1536], "uint8"),
    "w2q": ("sbuf", [128, 256], "float8_e4m3fn_x4"),
    "w2s": ("sbuf", [128, 256], "uint8"),
    "w1qi": ("sbuf", [128, 1024], "float8_e4m3fn_x4"),
    "w1si": ("sbuf", [128, 1024], "uint8"),
    "xqi": ("sbuf", [128, 1024], "float8_e4m3fn_x4"),
    "xsi": ("sbuf", [128, 1024], "uint8"),
    "pout": ("sbuf", [128, 1024], "float32"),
    "pin": ("sbuf", [128, 1024], "float32"),
    "zs": ("sbuf", [128, 1024], "float32"),
    "hb": ("sbuf", [128, 1024], "bfloat16"),
    "hq": ("sbuf", [128, 256], "float8_e4m3fn_x4"),
    "hs": ("sbuf", [128, 256], "uint8"),
    "hqi": ("sbuf", [128, 256], "float8_e4m3fn_x4"),
    "hsi": ("sbuf", [128, 256], "uint8"),
    "yb": ("sbuf", [128, 256], "float32"),
    "zp": ("psum", [128, 4096], "float32"),
}
SEMAPHORES = (
    ["lWA", "lWB", "lXPk", "lXPn", "lXPp", "lXOk", "lXOn", "lXOp", "lW2"]
    + ["qWA", "qWB", "qXPk", "qXP", "qXOk", "qXO", "qW2", "qH"]
    + ["hc", "hs", "w1left", "sent"]
    + ["aWA", "aWB", "aXP", "aXO", "aP0", "aP1", "aH"]
    + ["mP%d" % i for i in range(4)] + ["mO%d" % i for i in range(4)] + ["mY"]
    + ["cp%d" % i for i in range(4)] + ["zA%d" % i for i in range(4)]
    + ["hd", "yc", "sH", "sY"]
)


def _bits(mask):
    return [b for b in range(16) if (mask >> b) & 1]


def _mk(bits):
    m = 0
    for b in bits:
        m |= 1 << b
    return m


def _layout(T, topo):
    cores = list(T.cores)
    groups = []
    for r, c in enumerate(cores):
        for gl in groups:
            if topo.same_plane(topo.chip(cores[gl[0]]), topo.chip(c)):
                gl.append(r)
                break
        else:
            groups.append([r])
    ga, gb = groups
    partner = {}
    for r in ga:
        for s in gb:
            if s not in partner and topo.mates(topo.chip(cores[r]), topo.chip(cores[s])):
                partner[r] = s
                partner[s] = r
    rest_a = [r for r in ga if r not in partner]
    rest_b = [s for s in gb if s not in partner]
    for r, s in zip(rest_a, rest_b):
        partner[r] = s
        partner[s] = r
    nxt, prv = {}, {}
    for gl in groups:
        for q, r in enumerate(gl):
            nxt[r] = gl[(q + 1) % len(gl)]
            prv[r] = gl[(q + 2) % len(gl)]
    helpers = {}
    for r, c in enumerate(cores):
        cand = [d for d in range(topo.CORES_PER_CHIP * topo.CHIPS)
                if topo.chip(d) == topo.chip(c) and topo.die(d) != topo.die(c) and d not in cores
                and topo.may_write(d, cores[nxt[r]]) and topo.may_write(d, cores[prv[r]])]
        helpers[r] = cand[:2]
    return cores, partner, nxt, prv, helpers


def _tr(topo, dst_core, dst, src, mask, sem):
    rid, pid, _ = topo.addr(dst_core)
    return RemoteDMATransfer(dst_ids=[DstId(rid=rid, pnc=pid)], dma_engine_mask=mask, remote_sem=sem, src=src, dst=dst)


def _helper(g, core, T, topo, cores, n, p, piece):
    S = T.sem
    eng = _bits(topo.mask(core, cores[n]) & topo.mask(core, cores[p]))
    lo, hi = _mk(eng[:len(eng) // 2]), _mk(eng[len(eng) // 2:])
    arr = S["aWA"] if piece == 0 else S["aWB"]
    a = NC * piece
    g.wait_ge(S["hc"], 8)
    g.remote_dma_fused([
        _tr(topo, cores[n], T.w1qi[:, a:a + NC].bitcast(dt.uint8), T.w1qi[:, 0:NC].bitcast(dt.uint8), lo, arr),
        _tr(topo, cores[p], T.w1qi[:, 512 + a:512 + a + NC].bitcast(dt.uint8), T.w1qi[:, 0:NC].bitcast(dt.uint8), hi, arr),
    ], local_sem=S["sent"])
    g.wait_ge(S["hs"], 8)
    g.remote_dma_fused([
        _tr(topo, cores[n], T.w1si[:, a:a + NC], T.w1si[:, 0:NC], lo, arr),
        _tr(topo, cores[p], T.w1si[:, 512 + a:512 + a + NC], T.w1si[:, 0:NC], hi, arr),
    ], local_sem=S["sent"])
    g.wait_ge(S["sent"], 2 * len(eng))


def rank_program(g, core, T, topo):
    cores, partner, nxt, prv, helpers = _layout(T, topo)
    k = T.rank_of(core)
    if k is None:
        for r in range(len(cores)):
            if core in helpers[r]:
                _helper(g, core, T, topo, cores, nxt[r], prv[r], helpers[r].index(core))
        return
    S = T.sem
    N = len(cores)
    n, p, q = nxt[k], prv[k], partner[k]
    v, te, sc, sy = g.vector, g.tensor, g.scalar, g.sync

    def ldx(queue, c, sem):
        queue.dma_start(T.xb[:, 1024 * c:1024 * c + 1024], T.x[:, 1024 * c:1024 * c + 1024]).then_inc(S[sem], 16)

    sy.dma_start(T.w1b[:, 0:1024], T.w1[:, 0:1024]).then_inc(S["lWA"], 16)
    sc.dma_start(T.w1b[:, 1024:2048], T.w1[:, 1024:2048]).then_inc(S["lWB"], 16)
    ldx(sy, q, "lXPk")
    ldx(sc, partner[n], "lXPn")
    ldx(sy, partner[p], "lXPp")
    ldx(sc, k, "lXOk")
    sy.wait_ge(S["w1left"], 32)
    sc.wait_ge(S["w1left"], 32)
    ldx(sy, n, "lXOn")
    ldx(sc, p, "lXOp")
    sy.dma_start(T.w2b[:], T.w2[:]).then_inc(S["lW2"], 16)

    def qw1(i, sem):
        v.quantize_mx(T.w1q[:, 128 * i:128 * i + 128], T.w1s[:, 128 * i:128 * i + 128],
                      T.w1b[:, 512 * i:512 * i + 512]).then_inc(S[sem], 1)

    def qx(c, sem):
        v.quantize_mx(T.xq[:, NC * c:NC * c + NC], T.xs[:, NC * c:NC * c + NC],
                      T.xb[:, 1024 * c:1024 * c + 1024]).then_inc(S[sem], 1)

    v.wait_ge(S["lWA"], 16)
    qw1(0, "qWA")
    qw1(1, "qWA")
    v.wait_ge(S["lWB"], 16)
    qw1(2, "qWB")
    qw1(3, "qWB")
    v.wait_ge(S["lXPk"], 16)
    qx(q, "qXPk")
    v.wait_ge(S["lXPn"], 16)
    qx(partner[n], "qXP")
    v.wait_ge(S["lXPp"], 16)
    qx(partner[p], "qXP")
    v.wait_ge(S["lXOk"], 16)
    qx(k, "qXOk")
    v.wait_ge(S["lXOn"], 16)
    qx(n, "qXO")
    v.wait_ge(S["lXOp"], 16)
    qx(p, "qXO")

    off = topo.mask(core, cores[n]) & topo.mask(core, cores[p])
    eng = _bits(off)
    lo, hi = _mk(eng[:len(eng) // 2]), _mk(eng[len(eng) // 2:])
    for piece, sem in ((0, "qWA"), (1, "qWB")):
        hcore = helpers[k][piece]
        push = topo.mask(core, hcore) & ~off
        rid, pid, _ = topo.addr(hcore)
        a = NC * piece
        g.wait_ge(S[sem], 2)
        g.remote_dma(out_ap=T.w1qi[:, 0:NC].bitcast(dt.uint8), in_ap=T.w1q[:, a:a + NC].bitcast(dt.uint8),
                     remote_sem=S["hc"], local_sem=S["w1left"], pid=pid, routing_id=rid, dma_engine_mask=push)
        g.remote_dma(out_ap=T.w1si[:, 0:NC], in_ap=T.w1s[:, a:a + NC],
                     remote_sem=S["hs"], local_sem=S["w1left"], pid=pid, routing_id=rid, dma_engine_mask=push)

    def send_x(grp, cn, cp, arr):
        d0, d1 = NC * (2 * grp), NC * (2 * grp + 1)
        g.remote_dma_fused([
            _tr(topo, cores[n], T.xqi[:, d0:d0 + NC].bitcast(dt.uint8), T.xq[:, NC * cn:NC * cn + NC].bitcast(dt.uint8), lo, S[arr]),
            _tr(topo, cores[p], T.xqi[:, d1:d1 + NC].bitcast(dt.uint8), T.xq[:, NC * cp:NC * cp + NC].bitcast(dt.uint8), hi, S[arr]),
        ], local_sem=S["sent"])
        g.remote_dma_fused([
            _tr(topo, cores[n], T.xsi[:, d0:d0 + NC], T.xs[:, NC * cn:NC * cn + NC], lo, S[arr]),
            _tr(topo, cores[p], T.xsi[:, d1:d1 + NC], T.xs[:, NC * cp:NC * cp + NC], hi, S[arr]),
        ], local_sem=S["sent"])

    g.wait_ge(S["qXP"], 2)
    send_x(0, partner[n], partner[p], "aXP")
    g.wait_ge(S["qXO"], 2)
    send_x(1, n, p, "aXO")

    def mm(bank, wq, ws, wc, xq, xs, xc, start, stop):
        return te.matmul_mx(T.zp[:, 512 * bank:512 * bank + NC], wq[:, wc:wc + 128], ws[:, wc:wc + 128],
                            xq[:, xc:xc + NC], xs[:, xc:xc + NC], start, stop)

    te.wait_ge(S["qWA"], 2)
    te.wait_ge(S["qWB"], 2)
    te.wait_ge(S["qXPk"], 1)
    for i in range(4):
        mm(i, T.w1q, T.w1s, 128 * i, T.xq, T.xs, NC * q, True, False)
    te.wait_ge(S["qXOk"], 1)
    for i in range(4):
        mm(4 + i, T.w1q, T.w1s, 128 * i, T.xq, T.xs, NC * k, True, False)
    te.wait_ge(S["aXP"], 16)
    for piece, arr in ((0, "aWA"), (1, "aWB")):
        te.wait_ge(S[arr], 16)
        for i in (2 * piece, 2 * piece + 1):
            mm(i, T.w1qi, T.w1si, 128 * i, T.xqi, T.xsi, 0, False, False)
            mm(i, T.w1qi, T.w1si, 512 + 128 * i, T.xqi, T.xsi, NC, False, True).then_inc(S["mP%d" % i], 1)
    te.wait_ge(S["aXO"], 16)
    for i in range(4):
        mm(4 + i, T.w1qi, T.w1si, 128 * i, T.xqi, T.xsi, 2 * NC, False, False)
        mm(4 + i, T.w1qi, T.w1si, 512 + 128 * i, T.xqi, T.xsi, 3 * NC, False, True).then_inc(S["mO%d" % i], 1)

    for i in range(4):
        src, dst = T.zp[:, 512 * i:512 * i + NC], T.pout[:, NC * i:NC * i + NC]
        if i % 2 == 0:
            v.wait_ge(S["mP%d" % i], 1)
            v.tensor_copy(dst, src).then_inc(S["cp%d" % i], 1)
        else:
            sc.wait_ge(S["mP%d" % i], 1)
            sc.activation(dst, src, ActivationFunctionType.Copy).then_inc(S["cp%d" % i], 1)
    rid, pid, _ = topo.addr(cores[q])
    mq = topo.mask(core, cores[q])
    for piece in range(2):
        g.wait_ge(S["cp%d" % (2 * piece)], 1)
        g.wait_ge(S["cp%d" % (2 * piece + 1)], 1)
        a = 2 * NC * piece
        g.remote_dma(out_ap=T.pin[:, a:a + 2 * NC], in_ap=T.pout[:, a:a + 2 * NC], remote_sem=S["aP%d" % piece],
                     local_sem=S["sent"], pid=pid, routing_id=rid, dma_engine_mask=mq)

    v.wait_ge(S["lW2"], 16)
    for i in range(2):
        v.quantize_mx(T.w2q[:, 128 * i:128 * i + 128], T.w2s[:, 128 * i:128 * i + 128],
                      T.w2b[:, 512 * i:512 * i + 512]).then_inc(S["qW2"], 1)

    nq = len(_bits(mq))
    for i in range(4):
        v.wait_ge(S["mO%d" % i], 1)
        v.wait_ge(S["aP%d" % (i // 2)], nq)
        v.tensor_tensor(T.zs[:, NC * i:NC * i + NC], T.zp[:, 512 * (4 + i):512 * (4 + i) + NC],
                        T.pin[:, NC * i:NC * i + NC], AluOpType.add).then_inc(S["zA%d" % i], 1)
        sc.wait_ge(S["zA%d" % i], 1)
        sc.activation(T.hb[:, i:4 * NC:4], T.zs[:, NC * i:NC * i + NC], ActivationFunctionType.Relu,
                      scale=CACT).then_inc(S["hd"], 1)
    v.wait_ge(S["hd"], 4)
    v.quantize_mx(T.hq[:], T.hs[:], T.hb[:]).then_inc(S["qH"], 1)
    sy.wait_ge(S["hd"], 4)
    sy.dma_start(T.h[:], T.hb[:]).then_inc(S["sH"], 16)

    t = (k - 1) % N
    rid, pid, _ = topo.addr(cores[t])
    mt = topo.mask(core, cores[t])
    g.wait_ge(S["qH"], 1)
    g.remote_dma(out_ap=T.hqi[:].bitcast(dt.uint8), in_ap=T.hq[:].bitcast(dt.uint8), remote_sem=S["aH"],
                 local_sem=S["sent"], pid=pid, routing_id=rid, dma_engine_mask=mt)
    g.remote_dma(out_ap=T.hsi[:], in_ap=T.hs[:], remote_sem=S["aH"],
                 local_sem=S["sent"], pid=pid, routing_id=rid, dma_engine_mask=mt)
    g.wait_ge(S["sent"], 4 * len(eng) + 2 * nq + 2 * len(_bits(mt)))

    te.wait_ge(S["qW2"], 2)
    te.wait_ge(S["qH"], 1)
    te.wait_ge(S["cp0"], 1)
    te.matmul_mx(T.zp[:, 0:NC], T.w2q[:, 0:128], T.w2s[:, 0:128], T.hq[:], T.hs[:], True, False)
    te.wait_ge(S["aH"], 2 * len(_bits(topo.mask(cores[(k + 1) % N], core))))
    te.matmul_mx(T.zp[:, 0:NC], T.w2q[:, 128:256], T.w2s[:, 128:256], T.hqi[:], T.hsi[:], False, True).then_inc(S["mY"], 1)
    v.wait_ge(S["mY"], 1)
    v.tensor_copy(T.yb[:], T.zp[:, 0:NC]).then_inc(S["yc"], 1)
    sy.wait_ge(S["yc"], 1)
    sy.dma_start(T.y[:], T.yb[:]).then_inc(S["sY"], 16)
    sy.wait_ge(S["sH"], 16)
    sy.wait_ge(S["sY"], 16)
